import numpy as np
import ml_dtypes


def mxq(x, axis, fmt="e4m3"):
    dtype, down = {"e4m3": (ml_dtypes.float8_e4m3fn, 7), "e5m2": (ml_dtypes.float8_e5m2, 14)}[fmt]
    v = np.moveaxis(np.asarray(x, np.float32).astype(ml_dtypes.bfloat16).astype(np.float64), axis, -1)
    blocks = v.reshape(v.shape[:-1] + (-1, 32))
    amax = np.abs(blocks).max(-1, keepdims=True)
    byte = np.maximum(np.where(amax > 0, np.frexp(amax)[1] - 1 + 127, 0) - down, 1)
    scale = np.exp2(byte - 127.0)
    codes = (blocks / scale).astype(np.float32).astype(dtype).astype(np.float64)
    return np.moveaxis((codes * scale).reshape(v.shape), -1, axis)


WIDE = False


def mx_kscale(k):
    if not WIDE:
        return np.ones(k)
    levels = np.array([10, -10, 5, -5, 0])
    if k % 512:
        return np.exp2(np.random.permutation(np.resize(levels, k // 32))).repeat(32)
    a = np.empty((k // 512, 16))
    for p in range(k // 512):
        a[p, :8] = np.random.permutation(np.resize(levels, 8))
        for g in range(8):
            far = levels[np.abs(levels - a[p, g]) >= 10]
            a[p, g + 8] = far[np.random.randint(len(far))]
    return np.exp2(a.ravel()).repeat(32)


def f64(x):
    return np.asarray(x).astype(np.float64)


def striped(idx):
    return np.tile(np.asarray(idx).reshape(-1, 16).T, (8, 1)).astype(np.uint16)


def unstriped(offs):
    return offs[:16].T.reshape(-1).astype(np.int64)


B, N, T, D, DV, NQ = 2, 512, 2048, 512, 512, 128
PAGE = 64
NEW = 256


def setup_inputs():
    n = np.random.standard_normal
    pages = np.random.permutation(T // PAGE)[:B * N // PAGE]
    idx = (pages[:, None] * PAGE + np.arange(PAGE)[None, :]).reshape(-1)
    s = mx_kscale(D)[:, None]
    u = np.ones(T)
    u[idx] = mx_kscale(B * N)
    r = np.random.uniform(0.5, 2.0, T)
    raw = n((D, T)) / s / (u * r)
    new = np.random.permutation(idx.reshape(B, N)[:, -NEW // B:].reshape(-1))
    return {
        "qT": (n((B, D, NQ)) * s * (0.70 / np.sqrt(D))).astype(np.float32),
        "cT": np.where(np.isin(np.arange(T), new)[None, :], n((D, T)), raw).astype(np.float32),
        "new_cT": raw[:, new].astype(np.float32),
        "ts": np.tile(u * r, (128, 1)).astype(np.float32),
        "ch": np.tile(s[:, 0] * np.random.uniform(0.5, 2.0, D), (128, 1)).astype(np.float32),
        "offs": striped(idx),
        "slots": striped(new),
    }


def reference(qT, cT, new_cT, ts, ch, offs, slots):
    idx = unstriped(offs)
    c = f64(cT)
    c[:, unstriped(slots)] = f64(new_cT)
    pick = lambda x: x[:, idx].reshape(x.shape[0], B, N).transpose(1, 0, 2)
    q = f64(qT)
    score = mxq(q, 1, "e4m3").transpose(0, 2, 1) @ mxq(pick(c), 1, "e4m3")
    score = score * pick(f64(ts))[:, :1, :]
    m = score.max(-1, keepdims=True)
    p = np.exp(score - m)
    total = p.sum(-1, keepdims=True)
    w = p * pick(f64(ts))[:, :1, :]
    y = mxq(w, 2, "e4m3") @ mxq(pick(c).transpose(0, 2, 1), 1, "e4m3")
    y = y / total
    y = y * f64(ch)[:1]
    return y

@@ -1,0 +1,185 @@
+from contextlib import ExitStack
+
+import concourse.mybir as mybir
+from concourse.masks import make_identity
+
+B, N, T, D, NQ, NEW = 2, 512, 2048, 512, 128, 256
+P = 128
+PACK = 4
+FLOPS = 2 * 2 * B * NQ * N * D
+
+F32 = mybir.dt.float32
+BF16 = mybir.dt.bfloat16
+U32 = mybir.dt.uint32
+U16 = mybir.dt.uint16
+U8 = mybir.dt.uint8
+FP8X4 = mybir.dt.float8_e4m3fn_x4
+MULT = mybir.AluOpType.mult
+MIN = mybir.AluOpType.min
+EXP = mybir.ActivationFunctionType.Exp
+X = mybir.AxisListType.X
+
+
+def tile_attend_mla_append256_kernel(tc, qT, cT, new_cT, ts, ch, offs, slots, out):
+    nc = tc.nc
+    with ExitStack() as ctx:
+        keep = ctx.enter_context(tc.tile_pool(name="keep", bufs=1))
+        ps_v = ctx.enter_context(tc.psum_pool(name="ps_v", bufs=4))
+        ps_m = ctx.enter_context(tc.psum_pool(name="ps_m", bufs=2))
+        ps_w = ctx.enter_context(tc.psum_pool(name="ps_w", bufs=2))
+
+        place = keep.tile([P, NEW // 16], U16, name="place")
+        index = keep.tile([P, B * N // 16], U16, name="index")
+        plane = [keep.tile([P, T], F32, name=f"plane{t}") for t in range(PACK)]
+        fresh = [keep.tile([P, NEW], F32, name=f"fresh{t}") for t in range(PACK)]
+        q_raw = keep.tile([P, B, PACK, NQ], F32, name="q_raw")
+        ts_sb = keep.tile([P, T], F32, name="ts_sb")
+        ch_sb = keep.tile([P, D], F32, name="ch_sb")
+
+        cT_v = cT.rearrange("(p j) w -> p j w", j=PACK)
+        new_v = new_cT.rearrange("(p j) w -> p j w", j=PACK)
+        nc.sync.dma_start(place[:], slots)
+        for t in range(PACK):
+            nc.sync.dma_start(fresh[t][:], new_v[:, t, :])
+            if t == 1:
+                nc.sync.dma_start(index[:], offs)
+            if t == 3:
+                nc.sync.dma_start(q_raw[:], qT.rearrange("b (p j) q -> p b j q", j=PACK))
+            nc.sync.dma_start(plane[t][:], cT_v[:, t, :])
+        nc.sync.dma_start(ts_sb[:], ts)
+        nc.sync.dma_start(ch_sb[:], ch)
+
+        ident = keep.tile([P, P], F32, name="ident")
+        make_identity(nc, ident[:])
+        warm = keep.tile([P, 1], F32, name="warm")
+        warm2 = keep.tile([P, 1], F32, name="warm2")
+        nc.vector.memset(warm[:], 0.0)
+        nc.scalar.activation(warm2[:], warm[:], EXP)
+
+        g = [keep.tile([P, PACK, N], F32, name=f"g{b}") for b in range(B)]
+        kb = [keep.tile([P, N, PACK], BF16, name=f"kb{b}", align_bytes=64) for b in range(B)]
+        vb = [keep.tile([P, D, PACK], BF16, name=f"vb{b}", align_bytes=64) for b in range(B)]
+        kc = [keep.tile([P, N], U32, name=f"kc{b}", align_bytes=64) for b in range(B)]
+        ks = [keep.tile([P, N], U8, name=f"ks{b}", align_bytes=64) for b in range(B)]
+        vc = [keep.tile([P, D], U32, name=f"vc{b}", align_bytes=64) for b in range(B)]
+        vs = [keep.tile([P, D], U8, name=f"vs{b}", align_bytes=64) for b in range(B)]
+        tsg = [keep.tile([P, N], F32, name=f"tsg{b}") for b in range(B)]
+        qb = keep.tile([P, B, NQ, PACK], BF16, name="qb", align_bytes=64)
+        qc = keep.tile([P, B * NQ], U32, name="qc", align_bytes=64)
+        qs = keep.tile([P, B * NQ], U8, name="qs", align_bytes=64)
+
+        def lst(b):
+            return index[:, b * (N // 16) : (b + 1) * (N // 16)]
+
+        def scatter(t):
+            nc.vector.tensor_copy(plane[t][:].indirect(place[:]), fresh[t][:])
+
+        def gather(b, t):
+            nc.vector.tensor_copy(g[b][:, t, :], plane[t][:].indirect(lst(b)))
+
+        def turn(b, t):
+            bank = ps_v.tile([P, PACK, P], F32, name="turned")
+            view = g[b][:, t, :].rearrange("p (m j) -> p j m", j=PACK)
+            for j in range(PACK):
+                nc.tensor.transpose(bank[:, j, :], view[:, j, :], ident[:])
+            nc.scalar.copy(vb[b][:, t * P : (t + 1) * P, :], bank[:].rearrange("m j p -> m p j"))
+
+        def pair(b, h, engine):
+            dst = kb[b][:, :, 2 * h : 2 * h + 2]
+            src = g[b][:, 2 * h : 2 * h + 2, :].rearrange("p t n -> p n t")
+            if engine == "v":
+                nc.vector.tensor_copy(dst, src)
+            else:
+                nc.scalar.copy(dst, src)
+
+        def quant(codes, scales, src):
+            nc.vector.quantize_mx(out=codes.bitcast(FP8X4), scales=scales, in_=src)
+
+        def queries():
+            for b in range(B):
+                nc.scalar.copy(qb[:, b, :, :], q_raw[:, b, :, :].rearrange("p j q -> p q j"))
+            quant(qc[:], qs[:], qb[:].rearrange("p b q j -> p (b q j)"))
+
+        def scores(b):
+            quant(kc[b][:], ks[b][:], kb[b][:].rearrange("p n j -> p (n j)"))
+            bank = ps_m.tile([P, N], F32, name="mm")
+            nc.tensor.matmul_mx(
+                out=bank[:],
+                lhsT=qc[:, b * NQ : (b + 1) * NQ].bitcast(FP8X4),
+                lhsT_scale=qs[:, b * NQ : (b + 1) * NQ],
+                rhs=kc[b][:].bitcast(FP8X4),
+                rhs_scale=ks[b][:],
+                start=True,
+                stop=True,
+            )
+            return bank
+
+        def weights(b, bank):
+            neg_a = keep.tile([P, N], F32, name=f"neg_a{b}")
+            neg_m = keep.tile([P, 1], F32, name=f"neg_m{b}")
+            p = keep.tile([P, N], F32, name=f"p{b}")
+            total = keep.tile([P, 1], F32, name=f"total{b}")
+            recip = keep.tile([P, 1], F32, name=f"recip{b}")
+            w = keep.tile([P, N], BF16, name=f"w{b}", align_bytes=64)
+            nc.vector.scalar_tensor_tensor(neg_a[:], bank[:], -1.0, tsg[b][:], MULT, MULT)
+            nc.vector.tensor_reduce(neg_m[:], neg_a[:], X, MIN)
+            nc.scalar.activation(p[:], neg_a[:], EXP, bias=neg_m[:], scale=-1.0, accum_out=total[:])
+            nc.vector.tensor_tensor(w[:], p[:], tsg[b][:], MULT)
+            nc.vector.reciprocal(recip[:], total[:])
+            return w, recip
+
+        def product(b, w, recip):
+            turned_w = ps_w.tile([P, 2, P], F32, name="turned_w")
+            words = w[:].bitcast(F32).rearrange("q (m u) -> q u m", u=2)
+            for u in range(2):
+                nc.tensor.transpose(turned_w[:, u, :], words[:, u, :], ident[:])
+            wb = keep.tile([P, NQ, PACK], BF16, name=f"wb{b}", align_bytes=64)
+            wb_flat = wb[:].rearrange("m q j -> m (q j)")
+            nc.scalar.copy(wb_flat.bitcast(F32).rearrange("m (q u) -> m q u", u=2), turned_w[:].rearrange("m u q -> m q u"))
+            wc = keep.tile([P, NQ], U32, name=f"wc{b}", align_bytes=64)
+            ws = keep.tile([P, NQ], U8, name=f"ws{b}", align_bytes=64)
+            quant(wc[:], ws[:], wb_flat)
+            bank = ps_m.tile([P, D], F32, name="mm")
+            nc.tensor.matmul_mx(
+                out=bank[:],
+                lhsT=wc[:].bitcast(FP8X4),
+                lhsT_scale=ws[:],
+                rhs=vc[b][:].bitcast(FP8X4),
+                rhs_scale=vs[b][:],
+                start=True,
+                stop=True,
+            )
+            y = keep.tile([P, P, PACK], F32, name=f"y{b}")
+            nc.vector.scalar_tensor_tensor(
+                y[:], bank[:].rearrange("q (t p) -> q p t", t=PACK), recip[:],
+                ch_sb[:].rearrange("q (p t) -> q p t", t=PACK), MULT, MULT,
+            )
+            nc.sync.dma_start(out[b], y[:].rearrange("q p t -> q (p t)"))
+
+        def quant_v(b):
+            quant(vc[b][:], vs[b][:], vb[b][:].rearrange("m c j -> m (c j)"))
+
+        for t in range(PACK):
+            scatter(t)
+            gather(0, t)
+            turn(0, t)
+            if t == 1:
+                pair(0, 0, "s")
+        queries()
+        pair(0, 1, "v")
+        bank0 = scores(0)
+        for t in range(PACK):
+            gather(1, t)
+            turn(1, t)
+            if t == 1:
+                pair(1, 0, "s")
+        nc.vector.tensor_copy(tsg[0][:], ts_sb[:].indirect(lst(0)))
+        w0, recip0 = weights(0, bank0)
+        nc.vector.tensor_copy(tsg[1][:], ts_sb[:].indirect(lst(1)))
+        pair(1, 1, "v")
+        bank1 = scores(1)
+        quant_v(0)
+        product(0, w0, recip0)
+        w1, recip1 = weights(1, bank1)
+        quant_v(1)
+        product(1, w1, recip1)

@@ -33,20 +33,21 @@ def tile_attend_mla_append256_kernel(tc, qT, cT, new_cT, ts, ch, offs, slots, ou
         plane = [keep.tile([P, T], F32, name=f"plane{t}") for t in range(PACK)]
         fresh = [keep.tile([P, NEW], F32, name=f"fresh{t}") for t in range(PACK)]
         q_raw = keep.tile([P, B, PACK, NQ], F32, name="q_raw")
+        ts_row = keep.tile([P, T // P], F32, name="ts_row")
         ts_sb = keep.tile([P, T], F32, name="ts_sb")
         ch_sb = keep.tile([P, D], F32, name="ch_sb")
 
         cT_v = cT.rearrange("(p j) w -> p j w", j=PACK)
         new_v = new_cT.rearrange("(p j) w -> p j w", j=PACK)
+        nc.scalar.dma_start(ts_row[:], ts[0].rearrange("(p j) -> p j", p=P))
         nc.sync.dma_start(place[:], slots)
         for t in range(PACK):
             nc.sync.dma_start(fresh[t][:], new_v[:, t, :])
-            if t == 1:
-                nc.sync.dma_start(index[:], offs)
             if t == 3:
                 nc.sync.dma_start(q_raw[:], qT.rearrange("b (p j) q -> p b j q", j=PACK))
             nc.sync.dma_start(plane[t][:], cT_v[:, t, :])
-        nc.sync.dma_start(ts_sb[:], ts)
+            if t == 0:
+                nc.sync.dma_start(index[:], offs)
         nc.sync.dma_start(ch_sb[:], ch)
 
         ident = keep.tile([P, P], F32, name="ident")
@@ -56,41 +57,56 @@ def tile_attend_mla_append256_kernel(tc, qT, cT, new_cT, ts, ch, offs, slots, ou
         nc.vector.memset(warm[:], 0.0)
         nc.scalar.activation(warm2[:], warm[:], EXP)
 
-        g = [keep.tile([P, PACK, N], F32, name=f"g{b}") for b in range(B)]
+        g = [keep.tile([P, 2, B * N], F32, name=f"g{h}") for h in range(2)]
         kb = [keep.tile([P, N, PACK], BF16, name=f"kb{b}", align_bytes=64) for b in range(B)]
         vb = [keep.tile([P, D, PACK], BF16, name=f"vb{b}", align_bytes=64) for b in range(B)]
-        kc = [keep.tile([P, N], U32, name=f"kc{b}", align_bytes=64) for b in range(B)]
-        ks = [keep.tile([P, N], U8, name=f"ks{b}", align_bytes=64) for b in range(B)]
+        kc = keep.tile([P, B * N], U32, name="kc", align_bytes=64)
+        ks = keep.tile([P, B * N], U8, name="ks", align_bytes=64)
         vc = [keep.tile([P, D], U32, name=f"vc{b}", align_bytes=64) for b in range(B)]
         vs = [keep.tile([P, D], U8, name=f"vs{b}", align_bytes=64) for b in range(B)]
-        tsg = [keep.tile([P, N], F32, name=f"tsg{b}") for b in range(B)]
+        tsg = keep.tile([P, B * N], F32, name="tsg")
         qb = keep.tile([P, B, NQ, PACK], BF16, name="qb", align_bytes=64)
         qc = keep.tile([P, B * NQ], U32, name="qc", align_bytes=64)
         qs = keep.tile([P, B * NQ], U8, name="qs", align_bytes=64)
 
+        def spread_ts():
+            for k in range(4):
+                bank = ps_v.tile([P, 4, P], F32, name="turned")
+                for j in range(4):
+                    col = 4 * k + j
+                    nc.tensor.transpose(bank[:, j, :], ts_row[:, col : col + 1].to_broadcast([P, P]), ident[:])
+                dst = ts_sb[:].rearrange("i (p j) -> i p j", j=16)[:, :, 4 * k : 4 * k + 4]
+                nc.scalar.copy(dst, bank[:].rearrange("i j p -> i p j"))
+
         def lst(b):
             return index[:, b * (N // 16) : (b + 1) * (N // 16)]
+
+        def look_up_ts(b):
+            nc.vector.tensor_copy(tsg[:, b * N : (b + 1) * N], ts_sb[:].indirect(lst(b)))
 
         def scatter(t):
             nc.vector.tensor_copy(plane[t][:].indirect(place[:]), fresh[t][:])
 
-        def gather(b, t):
-            nc.vector.tensor_copy(g[b][:, t, :], plane[t][:].indirect(lst(b)))
+        def gather(t):
+            nc.vector.tensor_copy(g[t // 2][:, t % 2, :], plane[t][:].indirect(index[:]))
 
-        def turn(b, t):
-            bank = ps_v.tile([P, PACK, P], F32, name="turned")
-            view = g[b][:, t, :].rearrange("p (m j) -> p j m", j=PACK)
-            for j in range(PACK):
-                nc.tensor.transpose(bank[:, j, :], view[:, j, :], ident[:])
-            nc.scalar.copy(vb[b][:, t * P : (t + 1) * P, :], bank[:].rearrange("m j p -> m p j"))
+        def gather_one(b, t):
+            nc.vector.tensor_copy(g[t // 2][:, t % 2, b * N : (b + 1) * N], plane[t][:].indirect(lst(b)))
 
-        def pair(b, h, engine):
-            dst = kb[b][:, :, 2 * h : 2 * h + 2]
-            src = g[b][:, 2 * h : 2 * h + 2, :].rearrange("p t n -> p n t")
+        def pair(b, h, first, last, engine):
+            dst = kb[b][:, first:last, 2 * h : 2 * h + 2]
+            src = g[h][:, :, b * N + first : b * N + last].rearrange("p t n -> p n t")
             if engine == "v":
                 nc.vector.tensor_copy(dst, src)
             else:
                 nc.scalar.copy(dst, src)
+
+        def turn(b, t):
+            bank = ps_v.tile([P, PACK, P], F32, name="turned")
+            view = g[t // 2][:, t % 2, b * N : (b + 1) * N].rearrange("p (m j) -> p j m", j=PACK)
+            for j in range(PACK):
+                nc.tensor.transpose(bank[:, j, :], view[:, j, :], ident[:])
+            nc.scalar.copy(vb[b][:, t * P : (t + 1) * P, :], bank[:].rearrange("m j p -> m p j"))
 
         def quant(codes, scales, src):
             nc.vector.quantize_mx(out=codes.bitcast(FP8X4), scales=scales, in_=src)
@@ -101,85 +117,102 @@ def tile_attend_mla_append256_kernel(tc, qT, cT, new_cT, ts, ch, offs, slots, ou
             quant(qc[:], qs[:], qb[:].rearrange("p b q j -> p (b q j)"))
 
         def scores(b):
-            quant(kc[b][:], ks[b][:], kb[b][:].rearrange("p n j -> p (n j)"))
+            cols = slice(b * N, (b + 1) * N)
+            quant(kc[:, cols], ks[:, cols], kb[b][:].rearrange("p n j -> p (n j)"))
             bank = ps_m.tile([P, N], F32, name="mm")
             nc.tensor.matmul_mx(
                 out=bank[:],
                 lhsT=qc[:, b * NQ : (b + 1) * NQ].bitcast(FP8X4),
                 lhsT_scale=qs[:, b * NQ : (b + 1) * NQ],
-                rhs=kc[b][:].bitcast(FP8X4),
-                rhs_scale=ks[b][:],
+                rhs=kc[:, b * N : (b + 1) * N].bitcast(FP8X4),
+                rhs_scale=ks[:, b * N : (b + 1) * N],
                 start=True,
                 stop=True,
             )
             return bank
 
-        def weights(b, bank):
-            neg_a = keep.tile([P, N], F32, name=f"neg_a{b}")
-            neg_m = keep.tile([P, 1], F32, name=f"neg_m{b}")
-            p = keep.tile([P, N], F32, name=f"p{b}")
-            total = keep.tile([P, 1], F32, name=f"total{b}")
-            recip = keep.tile([P, 1], F32, name=f"recip{b}")
-            w = keep.tile([P, N], BF16, name=f"w{b}", align_bytes=64)
-            nc.vector.scalar_tensor_tensor(neg_a[:], bank[:], -1.0, tsg[b][:], MULT, MULT)
-            nc.vector.tensor_reduce(neg_m[:], neg_a[:], X, MIN)
-            nc.scalar.activation(p[:], neg_a[:], EXP, bias=neg_m[:], scale=-1.0, accum_out=total[:])
-            nc.vector.tensor_tensor(w[:], p[:], tsg[b][:], MULT)
-            nc.vector.reciprocal(recip[:], total[:])
-            return w, recip
+        neg_a = [keep.tile([P, N], F32, name=f"neg_a{b}") for b in range(B)]
+        neg_m = [keep.tile([P, 1], F32, name=f"neg_m{b}") for b in range(B)]
+        p = [keep.tile([P, N], F32, name=f"p{b}") for b in range(B)]
+        total = keep.tile([P, B], F32, name="total")
+        recip = keep.tile([P, B], F32, name="recip")
+        w = [keep.tile([P, N], BF16, name=f"w{b}", align_bytes=64) for b in range(B)]
+        wb = [keep.tile([P, NQ * PACK], BF16, name=f"wb{b}", align_bytes=64) for b in range(B)]
+        wc = [keep.tile([P, NQ], U32, name=f"wc{b}", align_bytes=64) for b in range(B)]
+        ws = [keep.tile([P, NQ], U8, name=f"ws{b}", align_bytes=64) for b in range(B)]
+        y = [keep.tile([P, P, PACK], F32, name=f"y{b}") for b in range(B)]
 
-        def product(b, w, recip):
+        def scale_and_max(b, bank):
+            nc.vector.scalar_tensor_tensor(neg_a[b][:], bank[:], -1.0, tsg[:, b * N : (b + 1) * N], MULT, MULT)
+            nc.vector.tensor_reduce(neg_m[b][:], neg_a[b][:], X, MIN)
+
+        def exp(b):
+            nc.scalar.activation(p[b][:], neg_a[b][:], EXP, bias=neg_m[b][:], scale=-1.0, accum_out=total[:, b : b + 1])
+
+        def weigh(b):
+            nc.vector.tensor_tensor(w[b][:], p[b][:], tsg[:, b * N : (b + 1) * N], MULT)
+
+        def turn_w(b):
             turned_w = ps_w.tile([P, 2, P], F32, name="turned_w")
-            words = w[:].bitcast(F32).rearrange("q (m u) -> q u m", u=2)
+            words = w[b][:].bitcast(F32).rearrange("q (m u) -> q u m", u=2)
             for u in range(2):
                 nc.tensor.transpose(turned_w[:, u, :], words[:, u, :], ident[:])
-            wb = keep.tile([P, NQ, PACK], BF16, name=f"wb{b}", align_bytes=64)
-            wb_flat = wb[:].rearrange("m q j -> m (q j)")
-            nc.scalar.copy(wb_flat.bitcast(F32).rearrange("m (q u) -> m q u", u=2), turned_w[:].rearrange("m u q -> m q u"))
-            wc = keep.tile([P, NQ], U32, name=f"wc{b}", align_bytes=64)
-            ws = keep.tile([P, NQ], U8, name=f"ws{b}", align_bytes=64)
-            quant(wc[:], ws[:], wb_flat)
+            nc.scalar.copy(wb[b][:].bitcast(F32).rearrange("m (q u) -> m q u", u=2), turned_w[:].rearrange("m u q -> m q u"))
+            quant(wc[b][:], ws[b][:], wb[b][:])
+
+        def product(b):
             bank = ps_m.tile([P, D], F32, name="mm")
             nc.tensor.matmul_mx(
                 out=bank[:],
-                lhsT=wc[:].bitcast(FP8X4),
-                lhsT_scale=ws[:],
+                lhsT=wc[b][:].bitcast(FP8X4),
+                lhsT_scale=ws[b][:],
                 rhs=vc[b][:].bitcast(FP8X4),
                 rhs_scale=vs[b][:],
                 start=True,
                 stop=True,
             )
-            y = keep.tile([P, P, PACK], F32, name=f"y{b}")
+            return bank
+
+        def finish(b, bank):
             nc.vector.scalar_tensor_tensor(
-                y[:], bank[:].rearrange("q (t p) -> q p t", t=PACK), recip[:],
+                y[b][:], bank[:].rearrange("q (t p) -> q p t", t=PACK), recip[:, b : b + 1],
                 ch_sb[:].rearrange("q (p t) -> q p t", t=PACK), MULT, MULT,
             )
-            nc.sync.dma_start(out[b], y[:].rearrange("q p t -> q (p t)"))
+            nc.sync.dma_start(out[b], y[b][:].rearrange("q p t -> q (p t)"))
 
-        def quant_v(b):
-            quant(vc[b][:], vs[b][:], vb[b][:].rearrange("m c j -> m (c j)"))
 
+        spread_ts()
         for t in range(PACK):
             scatter(t)
-            gather(0, t)
-            turn(0, t)
             if t == 1:
-                pair(0, 0, "s")
-        queries()
-        pair(0, 1, "v")
-        bank0 = scores(0)
+                for b in range(B):
+                    look_up_ts(b)
+            if t < 3:
+                gather(t)
+            else:
+                for b in range(B):
+                    gather_one(b, t)
+            for b in range(B):
+                if t == 1:
+                    pair(b, 0, 0, N, "s")
+                if t == 3:
+                    pair(b, 1, 0, 336, "v")
+                    pair(b, 1, 336, N, "s")
+            if t == 2:
+                queries()
+        banks = [scores(b) for b in range(B)]
+        for b in range(B):
+            scale_and_max(b, banks[b])
+            exp(b)
         for t in range(PACK):
-            gather(1, t)
-            turn(1, t)
-            if t == 1:
-                pair(1, 0, "s")
-        nc.vector.tensor_copy(tsg[0][:], ts_sb[:].indirect(lst(0)))
-        w0, recip0 = weights(0, bank0)
-        nc.vector.tensor_copy(tsg[1][:], ts_sb[:].indirect(lst(1)))
-        pair(1, 1, "v")
-        bank1 = scores(1)
-        quant_v(0)
-        product(0, w0, recip0)
-        w1, recip1 = weights(1, bank1)
-        quant_v(1)
-        product(1, w1, recip1)
+            for b in range(B):
+                turn(b, t)
+        products = []
+        for b in range(B):
+            weigh(b)
+            turn_w(b)
+            quant(vc[b][:], vs[b][:], vb[b][:].rearrange("m c j -> m (c j)"))
+            products.append(product(b))
+        nc.vector.reciprocal(recip[:], total[:])
+        for b in range(B):
+            finish(b, products[b])

from contextlib import ExitStack

import concourse.mybir as mybir
from concourse.masks import make_identity

B, N, T, D, NQ, NEW = 2, 512, 2048, 512, 128, 256
P = 128
PACK = 4
FLOPS = 2 * 2 * B * NQ * N * D

F32 = mybir.dt.float32
BF16 = mybir.dt.bfloat16
U32 = mybir.dt.uint32
U16 = mybir.dt.uint16
U8 = mybir.dt.uint8
FP8X4 = mybir.dt.float8_e4m3fn_x4
MULT = mybir.AluOpType.mult
MIN = mybir.AluOpType.min
EXP = mybir.ActivationFunctionType.Exp
X = mybir.AxisListType.X


def tile_attend_mla_append256_kernel(tc, qT, cT, new_cT, ts, ch, offs, slots, out):
    nc = tc.nc
    with ExitStack() as ctx:
        keep = ctx.enter_context(tc.tile_pool(name="keep", bufs=1))
        ps_v = ctx.enter_context(tc.psum_pool(name="ps_v", bufs=4))
        ps_m = ctx.enter_context(tc.psum_pool(name="ps_m", bufs=2))
        ps_w = ctx.enter_context(tc.psum_pool(name="ps_w", bufs=2))

        place = keep.tile([P, NEW // 16], U16, name="place")
        index = keep.tile([P, B * N // 16], U16, name="index")
        plane = [keep.tile([P, T], F32, name=f"plane{t}") for t in range(PACK)]
        fresh = [keep.tile([P, NEW], F32, name=f"fresh{t}") for t in range(PACK)]
        q_raw = keep.tile([P, B, PACK, NQ], F32, name="q_raw")
        ts_row = keep.tile([P, T // P], F32, name="ts_row")
        ts_sb = keep.tile([P, T], F32, name="ts_sb")
        ch_sb = keep.tile([P, D], F32, name="ch_sb")

        cT_v = cT.rearrange("(p j) w -> p j w", j=PACK)
        new_v = new_cT.rearrange("(p j) w -> p j w", j=PACK)
        nc.scalar.dma_start(ts_row[:], ts[0].rearrange("(p j) -> p j", p=P))
        nc.sync.dma_start(place[:], slots)
        for t in range(PACK):
            nc.sync.dma_start(fresh[t][:], new_v[:, t, :])
            if t == 3:
                nc.sync.dma_start(q_raw[:], qT.rearrange("b (p j) q -> p b j q", j=PACK))
            nc.sync.dma_start(plane[t][:], cT_v[:, t, :])
            if t == 0:
                nc.sync.dma_start(index[:], offs)
        nc.sync.dma_start(ch_sb[:], ch)

        ident = keep.tile([P, P], F32, name="ident")
        make_identity(nc, ident[:])
        warm = keep.tile([P, 1], F32, name="warm")
        warm2 = keep.tile([P, 1], F32, name="warm2")
        nc.vector.memset(warm[:], 0.0)
        nc.scalar.activation(warm2[:], warm[:], EXP)

        g = [keep.tile([P, 2, B * N], F32, name=f"g{h}") for h in range(2)]
        kb = [keep.tile([P, N, PACK], BF16, name=f"kb{b}", align_bytes=64) for b in range(B)]
        vb = [keep.tile([P, D, PACK], BF16, name=f"vb{b}", align_bytes=64) for b in range(B)]
        kc = keep.tile([P, B * N], U32, name="kc", align_bytes=64)
        ks = keep.tile([P, B * N], U8, name="ks", align_bytes=64)
        vc = [keep.tile([P, D], U32, name=f"vc{b}", align_bytes=64) for b in range(B)]
        vs = [keep.tile([P, D], U8, name=f"vs{b}", align_bytes=64) for b in range(B)]
        tsg = keep.tile([P, B * N], F32, name="tsg")
        qb = keep.tile([P, B, NQ, PACK], BF16, name="qb", align_bytes=64)
        qc = keep.tile([P, B * NQ], U32, name="qc", align_bytes=64)
        qs = keep.tile([P, B * NQ], U8, name="qs", align_bytes=64)

        def spread_ts():
            for k in range(4):
                bank = ps_v.tile([P, 4, P], F32, name="turned")
                for j in range(4):
                    col = 4 * k + j
                    nc.tensor.transpose(bank[:, j, :], ts_row[:, col : col + 1].to_broadcast([P, P]), ident[:])
                dst = ts_sb[:].rearrange("i (p j) -> i p j", j=16)[:, :, 4 * k : 4 * k + 4]
                nc.scalar.copy(dst, bank[:].rearrange("i j p -> i p j"))

        def lst(b):
            return index[:, b * (N // 16) : (b + 1) * (N // 16)]

        def look_up_ts(b):
            nc.vector.tensor_copy(tsg[:, b * N : (b + 1) * N], ts_sb[:].indirect(lst(b)))

        def scatter(t):
            nc.vector.tensor_copy(plane[t][:].indirect(place[:]), fresh[t][:])

        def gather(t):
            nc.vector.tensor_copy(g[t // 2][:, t % 2, :], plane[t][:].indirect(index[:]))

        def gather_one(b, t):
            nc.vector.tensor_copy(g[t // 2][:, t % 2, b * N : (b + 1) * N], plane[t][:].indirect(lst(b)))

        def pair(b, h, first, last, engine):
            dst = kb[b][:, first:last, 2 * h : 2 * h + 2]
            src = g[h][:, :, b * N + first : b * N + last].rearrange("p t n -> p n t")
            if engine == "v":
                nc.vector.tensor_copy(dst, src)
            else:
                nc.scalar.copy(dst, src)

        def turn(b, t):
            bank = ps_v.tile([P, PACK, P], F32, name="turned")
            view = g[t // 2][:, t % 2, b * N : (b + 1) * N].rearrange("p (m j) -> p j m", j=PACK)
            for j in range(PACK):
                nc.tensor.transpose(bank[:, j, :], view[:, j, :], ident[:])
            nc.scalar.copy(vb[b][:, t * P : (t + 1) * P, :], bank[:].rearrange("m j p -> m p j"))

        def quant(codes, scales, src):
            nc.vector.quantize_mx(out=codes.bitcast(FP8X4), scales=scales, in_=src)

        def queries():
            for b in range(B):
                nc.scalar.copy(qb[:, b, :, :], q_raw[:, b, :, :].rearrange("p j q -> p q j"))
            quant(qc[:], qs[:], qb[:].rearrange("p b q j -> p (b q j)"))

        def scores(b):
            cols = slice(b * N, (b + 1) * N)
            quant(kc[:, cols], ks[:, cols], kb[b][:].rearrange("p n j -> p (n j)"))
            bank = ps_m.tile([P, N], F32, name="mm")
            nc.tensor.matmul_mx(
                out=bank[:],
                lhsT=qc[:, b * NQ : (b + 1) * NQ].bitcast(FP8X4),
                lhsT_scale=qs[:, b * NQ : (b + 1) * NQ],
                rhs=kc[:, b * N : (b + 1) * N].bitcast(FP8X4),
                rhs_scale=ks[:, b * N : (b + 1) * N],
                start=True,
                stop=True,
            )
            return bank

        neg_a = [keep.tile([P, N], F32, name=f"neg_a{b}") for b in range(B)]
        neg_m = [keep.tile([P, 1], F32, name=f"neg_m{b}") for b in range(B)]
        p = [keep.tile([P, N], F32, name=f"p{b}") for b in range(B)]
        total = keep.tile([P, B], F32, name="total")
        recip = keep.tile([P, B], F32, name="recip")
        w = [keep.tile([P, N], BF16, name=f"w{b}", align_bytes=64) for b in range(B)]
        wb = [keep.tile([P, NQ * PACK], BF16, name=f"wb{b}", align_bytes=64) for b in range(B)]
        wc = [keep.tile([P, NQ], U32, name=f"wc{b}", align_bytes=64) for b in range(B)]
        ws = [keep.tile([P, NQ], U8, name=f"ws{b}", align_bytes=64) for b in range(B)]
        y = [keep.tile([P, P, PACK], F32, name=f"y{b}") for b in range(B)]

        def scale_and_max(b, bank):
            nc.vector.scalar_tensor_tensor(neg_a[b][:], bank[:], -1.0, tsg[:, b * N : (b + 1) * N], MULT, MULT)
            nc.vector.tensor_reduce(neg_m[b][:], neg_a[b][:], X, MIN)

        def exp(b):
            nc.scalar.activation(p[b][:], neg_a[b][:], EXP, bias=neg_m[b][:], scale=-1.0, accum_out=total[:, b : b + 1])

        def weigh(b):
            nc.vector.tensor_tensor(w[b][:], p[b][:], tsg[:, b * N : (b + 1) * N], MULT)

        def turn_w(b):
            turned_w = ps_w.tile([P, 2, P], F32, name="turned_w")
            words = w[b][:].bitcast(F32).rearrange("q (m u) -> q u m", u=2)
            for u in range(2):
                nc.tensor.transpose(turned_w[:, u, :], words[:, u, :], ident[:])
            nc.scalar.copy(wb[b][:].bitcast(F32).rearrange("m (q u) -> m q u", u=2), turned_w[:].rearrange("m u q -> m q u"))
            quant(wc[b][:], ws[b][:], wb[b][:])

        def product(b):
            bank = ps_m.tile([P, D], F32, name="mm")
            nc.tensor.matmul_mx(
                out=bank[:],
                lhsT=wc[b][:].bitcast(FP8X4),
                lhsT_scale=ws[b][:],
                rhs=vc[b][:].bitcast(FP8X4),
                rhs_scale=vs[b][:],
                start=True,
                stop=True,
            )
            return bank

        def finish(b, bank):
            nc.vector.scalar_tensor_tensor(
                y[b][:], bank[:].rearrange("q (t p) -> q p t", t=PACK), recip[:, b : b + 1],
                ch_sb[:].rearrange("q (p t) -> q p t", t=PACK), MULT, MULT,
            )
            nc.sync.dma_start(out[b], y[b][:].rearrange("q p t -> q (p t)"))


        spread_ts()
        for t in range(PACK):
            scatter(t)
            if t == 1:
                for b in range(B):
                    look_up_ts(b)
            if t < 3:
                gather(t)
            else:
                for b in range(B):
                    gather_one(b, t)
            for b in range(B):
                if t == 1:
                    pair(b, 0, 0, N, "s")
                if t == 3:
                    pair(b, 1, 0, 336, "v")
                    pair(b, 1, 336, N, "s")
            if t == 2:
                queries()
        banks = [scores(b) for b in range(B)]
        for b in range(B):
            scale_and_max(b, banks[b])
            exp(b)
        for t in range(PACK):
            for b in range(B):
                turn(b, t)
        products = []
        for b in range(B):
            weigh(b)
            turn_w(b)
            quant(vc[b][:], vs[b][:], vb[b][:].rearrange("m c j -> m (c j)"))
            products.append(product(b))
        nc.vector.reciprocal(recip[:], total[:])
        for b in range(B):
            finish(b, products[b])
